import numpy as np
import ml_dtypes


def mxq(x, axis, fmt="e4m3"):
    dtype, down = {"e4m3": (ml_dtypes.float8_e4m3fn, 7), "e5m2": (ml_dtypes.float8_e5m2, 14)}[fmt]
    v = np.moveaxis(np.asarray(x, np.float32).astype(ml_dtypes.bfloat16).astype(np.float64), axis, -1)
    blocks = v.reshape(v.shape[:-1] + (-1, 32))
    amax = np.abs(blocks).max(-1, keepdims=True)
    byte = np.maximum(np.where(amax > 0, np.frexp(amax)[1] - 1 + 127, 0) - down, 1)
    scale = np.exp2(byte - 127.0)
    codes = (blocks / scale).astype(np.float32).astype(dtype).astype(np.float64)
    return np.moveaxis((codes * scale).reshape(v.shape), -1, axis)


WIDE = False


def mx_kscale(k):
    if not WIDE:
        return np.ones(k)
    levels = np.array([10, -10, 5, -5, 0])
    if k % 512:
        return np.exp2(np.random.permutation(np.resize(levels, k // 32))).repeat(32)
    a = np.empty((k // 512, 16))
    for p in range(k // 512):
        a[p, :8] = np.random.permutation(np.resize(levels, 8))
        for g in range(8):
            far = levels[np.abs(levels - a[p, g]) >= 10]
            a[p, g + 8] = far[np.random.randint(len(far))]
    return np.exp2(a.ravel()).repeat(32)


def f64(x):
    return np.asarray(x).astype(np.float64)


def striped(idx):
    return np.tile(np.asarray(idx).reshape(-1, 16).T, (8, 1)).astype(np.uint16)


def unstriped(offs):
    return offs[:16].T.reshape(-1).astype(np.int64)


D, T, I, E = 512, 2048, 512, 512


def setup_inputs():
    n = np.random.standard_normal
    idx = np.random.permutation(T)[:I]
    fd = mx_kscale(D)
    fi = mx_kscale(I)
    return {
        "state": (n((D, E)) * 1 / np.sqrt(D) * fd[:, None]).astype(np.float32),
        "keys": (n((D, T)) / fd[:, None]).astype(np.float32),
        "vals": (n((E, T))).astype(np.float32),
        "step": (np.random.uniform(0.05, 0.2, (I, 1)) * fi[:, None]).astype(np.float32),
        "vsc": (np.random.uniform(0.5, 2.0, (I, 1)) / fi[:, None]).astype(np.float32),
        "dsc": (np.random.uniform(0.5, 2.0, (1, D)) * fd).astype(np.float32),
        "offs": striped(idx),
    }


def reference(state, keys, vals, step, vsc, dsc, offs):
    idx = unstriped(offs)
    stateq = mxq(f64(state), 0, "e4m3")
    keysidxq = mxq(f64(keys)[:, idx], 0, "e4m3")
    b = stateq.T @ keysidxq
    err = f64(vals)[:, idx] - b
    et = err.T
    es = et * f64(vsc)
    kt = f64(keys)[:, idx].T
    ks = kt * f64(step) * f64(dsc)
    ksq = mxq(ks, 0, "e4m3")
    esq = mxq(es, 0, "e4m3")
    y = ksq.T @ esq
    return y

@@ -1,0 +1,176 @@
+from contextlib import ExitStack
+
+import concourse.mybir as mybir
+from concourse.masks import make_identity
+
+D, T, I, E = 512, 2048, 512, 512
+FLOPS = 2 * D * I * E + 2 * I * D * E
+
+F32 = mybir.dt.float32
+BF16 = mybir.dt.bfloat16
+U32 = mybir.dt.uint32
+U16 = mybir.dt.uint16
+U8 = mybir.dt.uint8
+FP8X4 = mybir.dt.float8_e4m3fn_x4
+COPY = mybir.ActivationFunctionType.Copy
+MULT = mybir.AluOpType.mult
+
+P = 128
+PACK = 4
+RUN = 8
+HALF = 256
+
+
+def tile_attend_deltastep_kernel(tc, state, keys, vals, step, vsc, dsc, offs, out):
+    nc = tc.nc
+    with ExitStack() as ctx:
+        keep = ctx.enter_context(tc.tile_pool(name="keep", bufs=1))
+        psum = ctx.enter_context(tc.psum_pool(name="psum", bufs=1))
+
+        def held(name, shape, dtype):
+            return keep.tile(shape, dtype, name=name, align_bytes=64)
+
+        def gather(dst, window):
+            nc.vector.tensor_copy(
+                out=dst.bitcast(U32).rearrange("p (r g j) -> p g r j", r=PACK, j=RUN),
+                in_=window[:].bitcast(U32).indirect(offsets[:]),
+            )
+
+        def quantize(name, grouped, width):
+            codes = held(name + "_codes", [P, width], U32)
+            scales = held(name + "_scales", [P, width], U8)
+            nc.vector.quantize_mx(
+                out=codes[:].bitcast(FP8X4), scales=scales[:], in_=grouped[:].rearrange("p w j -> p (w j)")
+            )
+            return codes, scales
+
+        def product(acc, lhs, lhs_cols, rhs):
+            nc.tensor.matmul_mx(
+                out=acc,
+                lhsT=lhs[0][:, lhs_cols].bitcast(FP8X4),
+                lhsT_scale=lhs[1][:, lhs_cols],
+                rhs=rhs[0][:].bitcast(FP8X4),
+                rhs_scale=rhs[1][:],
+                start=True,
+                stop=True,
+            )
+
+        slot_rows = held("slot_rows", [P, P], F32)
+        nc.gpsimd.memset(slot_rows[:], 0.0)
+        dsc_cols = held("dsc_cols", [P, PACK], F32)
+        nc.scalar.dma_start(out=dsc_cols[:], in_=dsc.rearrange("o (p t) -> p (o t)", t=PACK))
+        for n, vec in enumerate((step, vsc)):
+            nc.scalar.dma_start(
+                out=slot_rows[n * PACK : (n + 1) * PACK, :].rearrange("r (g j) -> r g j", j=RUN),
+                in_=vec.rearrange("(g r j) o -> r g (j o)", r=PACK, j=RUN),
+            )
+        ident = held("ident", [P, P], F32)
+        make_identity(nc, ident[:])
+        offsets = keep.tile([P, I // 16], U16, name="offsets")
+        keys_planes = keys.rearrange("(p t) c -> t p c", t=PACK)
+        key_pool = [held(f"key_pool{t}", [P, T], F32) for t in range(PACK)]
+        val_pool = [held(f"val_pool{c}", [P, T], F32) for c in range(E // P)]
+        state_raw = [held(f"state_raw{h}", [P, PACK, HALF], F32) for h in range(2)]
+        state_rows = state.rearrange("(p t) e -> p t e", t=PACK)
+        nc.sync.dma_start(out=key_pool[0][:], in_=keys_planes[0])
+        nc.sync.dma_start(offsets[:], offs)
+        for t in range(1, PACK):
+            nc.sync.dma_start(out=key_pool[t][:], in_=keys_planes[t])
+        for c in range(E // P):
+            if c < 2:
+                nc.sync.dma_start(out=state_raw[c][:], in_=state_rows[:, :, c * HALF : (c + 1) * HALF])
+            nc.sync.dma_start(out=val_pool[c][:], in_=vals[c * P : (c + 1) * P, :])
+
+        turned = psum.tile([P, PACK, P], F32, name="slot_turn", tag="turn", bufs=4)
+        nc.tensor.transpose(turned[:, 0, :], slot_rows[:], ident[:])
+        slot_cols = held("slot_cols", [P, 2 * PACK], F32)
+        nc.scalar.copy(out=slot_cols[:], in_=turned[:, 0, 0 : 2 * PACK])
+        step_wide = slot_cols[:, 0:PACK].unsqueeze(1).to_broadcast([P, P, PACK])
+        vsc_wide = slot_cols[:, PACK : 2 * PACK].unsqueeze(1).to_broadcast([P, P, PACK])
+
+        picked = held("picked", [P, PACK, I], F32)
+        key_banks, ks_q = [], []
+
+        def turn_keys(t):
+            scaled = held(f"scaled{t}", [P, I], F32)
+            nc.scalar.activation(out=scaled[:], in_=picked[:, t, :], func=COPY, scale=dsc_cols[:, t : t + 1])
+            bank = psum.tile([P, PACK, P], F32, name=f"key_turn{t}", tag="turn", bufs=4)
+            for r in range(PACK):
+                nc.tensor.transpose(bank[:, r, :], scaled[:, r * P : (r + 1) * P], ident[:])
+            key_banks.append(bank)
+
+        def scale_and_quantize(name, bank, wide):
+            grouped = held(name, [P, P, PACK], BF16)
+            nc.vector.tensor_tensor(out=grouped[:], in0=bank[:].rearrange("s r x -> s x r"), in1=wide, op=MULT)
+            return quantize(name, grouped, P)
+
+        for t in range(PACK):
+            gather(picked[:, t, :], key_pool[t])
+            if t > 0:
+                ks_q.append(scale_and_quantize(f"ks{t - 1}", key_banks[t - 1], step_wide))
+            if t < PACK - 1:
+                turn_keys(t)
+
+        def interleave(copy, dst, src):
+            copy(out=dst.rearrange("p (c i) t -> p c t i", i=4), in_=src.rearrange("p t (c i) -> p c t i", i=4))
+
+        keys_grouped = held("keys_grouped", [P, I, PACK], BF16)
+        state_grouped = [held(f"state_grouped{h}", [P, HALF, PACK], BF16) for h in range(2)]
+        interleave(nc.scalar.copy, keys_grouped[:, 0:HALF, :], picked[:, :, 0:HALF])
+        turn_keys(PACK - 1)
+        interleave(nc.vector.tensor_copy, state_grouped[0][:], state_raw[0][:])
+        interleave(nc.vector.tensor_copy, keys_grouped[:, HALF:I, :], picked[:, :, HALF:I])
+        state_q = [quantize("state0", state_grouped[0], HALF)]
+        keys_q = quantize("keys", keys_grouped, I)
+
+        blocks = E // P
+        err_banks = []
+
+        def predict(c):
+            acc = psum.tile([P, I], F32, name=f"b{c}", tag="b", bufs=2)
+            product(acc[:], state_q[c // 2], slice(c % 2 * P, (c % 2 + 1) * P), keys_q)
+            neg = held(f"minus_b{c}", [P, I], F32)
+            nc.scalar.activation(out=neg[:], in_=acc[:], func=COPY, scale=-1.0)
+            bank = psum.tile([P, PACK, P], F32, name=f"err{c}", tag="turn", bufs=4)
+            err_banks.append((bank, neg))
+
+        def open_err(c):
+            bank, neg = err_banks[c]
+            for r in range(PACK):
+                nc.tensor.matmul(
+                    bank[:, r, :], neg[:, r * P : (r + 1) * P], ident[:], start=(r == 0), stop=False, is_transpose=True
+                )
+
+        def gather_vals(c):
+            picked_vals = held(f"picked_vals{c}", [P, I], F32)
+            gather(picked_vals[:], val_pool[c])
+            open_err(c)
+            for r in range(PACK):
+                nc.tensor.matmul(
+                    err_banks[c][0][:, r, :],
+                    picked_vals[:, r * P : (r + 1) * P],
+                    ident[:],
+                    start=False,
+                    stop=(r == PACK - 1),
+                    is_transpose=True,
+                )
+
+        out_rows = out.rearrange("(p t) e -> p t e", t=PACK)
+        predict(0)
+        predict(1)
+        gather_vals(0)
+        interleave(nc.scalar.copy, state_grouped[1][:], state_raw[1][:])
+        ks_q.append(scale_and_quantize(f"ks{PACK - 1}", key_banks[PACK - 1], step_wide))
+        state_q.append(quantize("state1", state_grouped[1], HALF))
+        predict(2)
+        predict(3)
+        for c in range(blocks):
+            if c + 1 < blocks:
+                gather_vals(c + 1)
+            es_q = scale_and_quantize(f"es{c}", err_banks[c][0], vsc_wide)
+            acc = psum.tile([P, PACK, P], F32, name=f"update{c}", tag="update", bufs=2)
+            for t in range(PACK):
+                product(acc[:, t, :], ks_q[t], slice(0, P), es_q)
+            result = held(f"result{c}", [P, PACK, P], F32)
+            nc.scalar.copy(out=result[:], in_=acc[:])
+            nc.sync.dma_start(out=out_rows[:, :, c * P : (c + 1) * P], in_=result[:])

@@ -19,16 +19,26 @@ P = 128
 PACK = 4
 RUN = 8
 HALF = 256
+POOL_BYTES = 4 * T
+GROUPED_BYTES = 2 * PACK * P
+STATE_BYTES = 4 * PACK * HALF
+KEY_AT = [0, POOL_BYTES, 2 * POOL_BYTES + STATE_BYTES, 3 * POOL_BYTES + STATE_BYTES]
+VAL_AT = [KEY_AT[3] + (1 + c) * POOL_BYTES for c in range(E // P)]
+STATE_AT = [2 * POOL_BYTES, VAL_AT[3] + POOL_BYTES]
+KEYS_GROUPED_AT = STATE_AT[1] + STATE_BYTES
 
 
 def tile_attend_deltastep_kernel(tc, state, keys, vals, step, vsc, dsc, offs, out):
     nc = tc.nc
     with ExitStack() as ctx:
         keep = ctx.enter_context(tc.tile_pool(name="keep", bufs=1))
+        placed = ctx.enter_context(tc.tile_pool(name="placed", bufs=1))
         psum = ctx.enter_context(tc.psum_pool(name="psum", bufs=1))
 
-        def held(name, shape, dtype):
-            return keep.tile(shape, dtype, name=name, align_bytes=64)
+        def held(name, shape, dtype, at=None):
+            if at is None:
+                return keep.tile(shape, dtype, name=name, align_bytes=64)
+            return placed.tile(shape, dtype, name=name, align_bytes=64, offset=at)
 
         def gather(dst, window):
             nc.vector.tensor_copy(
@@ -36,9 +46,9 @@ def tile_attend_deltastep_kernel(tc, state, keys, vals, step, vsc, dsc, offs, ou
                 in_=window[:].bitcast(U32).indirect(offsets[:]),
             )
 
-        def quantize(name, grouped, width):
+        def quantize(name, grouped, width, after=None):
             codes = held(name + "_codes", [P, width], U32)
-            scales = held(name + "_scales", [P, width], U8)
+            scales = held(name + "_scales", [P, width], U8, after)
             nc.vector.quantize_mx(
                 out=codes[:].bitcast(FP8X4), scales=scales[:], in_=grouped[:].rearrange("p w j -> p (w j)")
             )
@@ -57,28 +67,28 @@ def tile_attend_deltastep_kernel(tc, state, keys, vals, step, vsc, dsc, offs, ou
 
         slot_rows = held("slot_rows", [P, P], F32)
         nc.gpsimd.memset(slot_rows[:], 0.0)
-        dsc_cols = held("dsc_cols", [P, PACK], F32)
-        nc.scalar.dma_start(out=dsc_cols[:], in_=dsc.rearrange("o (p t) -> p (o t)", t=PACK))
-        for n, vec in enumerate((step, vsc)):
-            nc.scalar.dma_start(
-                out=slot_rows[n * PACK : (n + 1) * PACK, :].rearrange("r (g j) -> r g j", j=RUN),
-                in_=vec.rearrange("(g r j) o -> r g (j o)", r=PACK, j=RUN),
-            )
         ident = held("ident", [P, P], F32)
         make_identity(nc, ident[:])
         offsets = keep.tile([P, I // 16], U16, name="offsets")
         keys_planes = keys.rearrange("(p t) c -> t p c", t=PACK)
-        key_pool = [held(f"key_pool{t}", [P, T], F32) for t in range(PACK)]
-        val_pool = [held(f"val_pool{c}", [P, T], F32) for c in range(E // P)]
-        state_raw = [held(f"state_raw{h}", [P, PACK, HALF], F32) for h in range(2)]
+        key_pool = [held(f"key_pool{t}", [P, T], F32, KEY_AT[t]) for t in range(PACK)]
+        val_pool = [held(f"val_pool{c}", [P, T], F32, VAL_AT[c]) for c in range(E // P)]
+        state_raw = [held(f"state_raw{h}", [P, PACK, HALF], F32, STATE_AT[h]) for h in range(2)]
         state_rows = state.rearrange("(p t) e -> p t e", t=PACK)
         nc.sync.dma_start(out=key_pool[0][:], in_=keys_planes[0])
         nc.sync.dma_start(offsets[:], offs)
+        dsc_cols = held("dsc_cols", [P, PACK], F32)
+        nc.sync.dma_start(out=dsc_cols[:], in_=dsc.rearrange("o (p t) -> p (o t)", t=PACK))
+        for n, vec in enumerate((step, vsc)):
+            nc.sync.dma_start(
+                out=slot_rows[n * PACK : (n + 1) * PACK, :].rearrange("r (g j) -> r g j", j=RUN),
+                in_=vec.rearrange("(g r j) o -> r g (j o)", r=PACK, j=RUN),
+            )
         for t in range(1, PACK):
             nc.sync.dma_start(out=key_pool[t][:], in_=keys_planes[t])
+        for h in range(2):
+            nc.sync.dma_start(out=state_raw[h][:], in_=state_rows[:, :, h * HALF : (h + 1) * HALF])
         for c in range(E // P):
-            if c < 2:
-                nc.sync.dma_start(out=state_raw[c][:], in_=state_rows[:, :, c * HALF : (c + 1) * HALF])
             nc.sync.dma_start(out=val_pool[c][:], in_=vals[c * P : (c + 1) * P, :])
 
         turned = psum.tile([P, PACK, P], F32, name="slot_turn", tag="turn", bufs=4)
@@ -93,84 +103,106 @@ def tile_attend_deltastep_kernel(tc, state, keys, vals, step, vsc, dsc, offs, ou
 
         def turn_keys(t):
             scaled = held(f"scaled{t}", [P, I], F32)
-            nc.scalar.activation(out=scaled[:], in_=picked[:, t, :], func=COPY, scale=dsc_cols[:, t : t + 1])
+            if t < PACK - 1:
+                nc.scalar.activation(out=scaled[:], in_=picked[:, t, :], func=COPY, scale=dsc_cols[:, t : t + 1])
+            else:
+                nc.vector.tensor_scalar(
+                    out=scaled[:], in0=picked[:, t, :], scalar1=dsc_cols[:, t : t + 1], scalar2=None, op0=MULT
+                )
             bank = psum.tile([P, PACK, P], F32, name=f"key_turn{t}", tag="turn", bufs=4)
             for r in range(PACK):
                 nc.tensor.transpose(bank[:, r, :], scaled[:, r * P : (r + 1) * P], ident[:])
             key_banks.append(bank)
 
-        def scale_and_quantize(name, bank, wide):
-            grouped = held(name, [P, P, PACK], BF16)
+        def scale(name, bank, wide, at=None):
+            grouped = held(name, [P, P, PACK], BF16, at)
             nc.vector.tensor_tensor(out=grouped[:], in0=bank[:].rearrange("s r x -> s x r"), in1=wide, op=MULT)
-            return quantize(name, grouped, P)
+            return grouped
 
+        ks = []
         for t in range(PACK):
             gather(picked[:, t, :], key_pool[t])
+            if t > 1:
+                ks_q.append(quantize(f"ks{t - 2}", ks[t - 2], P, KEY_AT[t] + POOL_BYTES // 2))
+            turn_keys(t)
             if t > 0:
-                ks_q.append(scale_and_quantize(f"ks{t - 1}", key_banks[t - 1], step_wide))
-            if t < PACK - 1:
-                turn_keys(t)
+                ks.append(scale(f"ks{t - 1}", key_banks[t - 1], step_wide, KEY_AT[t]))
 
         def interleave(copy, dst, src):
             copy(out=dst.rearrange("p (c i) t -> p c t i", i=4), in_=src.rearrange("p t (c i) -> p c t i", i=4))
 
-        keys_grouped = held("keys_grouped", [P, I, PACK], BF16)
-        state_grouped = [held(f"state_grouped{h}", [P, HALF, PACK], BF16) for h in range(2)]
-        interleave(nc.scalar.copy, keys_grouped[:, 0:HALF, :], picked[:, :, 0:HALF])
-        turn_keys(PACK - 1)
+        keys_grouped = held("keys_grouped", [P, I, PACK], BF16, KEYS_GROUPED_AT)
+        state_grouped = [held(f"state_grouped{h}", [P, HALF, PACK], BF16, KEY_AT[2] if h == 0 else None) for h in range(2)]
+        interleave(nc.scalar.copy, keys_grouped[:], picked[:])
         interleave(nc.vector.tensor_copy, state_grouped[0][:], state_raw[0][:])
-        interleave(nc.vector.tensor_copy, keys_grouped[:, HALF:I, :], picked[:, :, HALF:I])
+        ks_q.append(quantize("ks2", ks[2], P, STATE_AT[0]))
         state_q = [quantize("state0", state_grouped[0], HALF)]
+        picked_vals = []
+
+        def gather_vals(c, at=None):
+            picked_vals.append(held(f"picked_vals{c}", [P, I], F32, at))
+            gather(picked_vals[c][:], val_pool[c])
+
         keys_q = quantize("keys", keys_grouped, I)
+        gather_vals(0, KEYS_GROUPED_AT)
+        interleave(nc.scalar.copy, state_grouped[1][:], state_raw[1][:])
 
         blocks = E // P
-        err_banks = []
+        minus_b, err_banks = [], []
 
         def predict(c):
             acc = psum.tile([P, I], F32, name=f"b{c}", tag="b", bufs=2)
             product(acc[:], state_q[c // 2], slice(c % 2 * P, (c % 2 + 1) * P), keys_q)
-            neg = held(f"minus_b{c}", [P, I], F32)
+            neg = held(f"minus_b{c}", [P, I], F32, STATE_AT[1] if c == 0 else None)
             nc.scalar.activation(out=neg[:], in_=acc[:], func=COPY, scale=-1.0)
+            minus_b.append(neg)
+
+        def turn_err(c):
             bank = psum.tile([P, PACK, P], F32, name=f"err{c}", tag="turn", bufs=4)
-            err_banks.append((bank, neg))
-
-        def open_err(c):
-            bank, neg = err_banks[c]
-            for r in range(PACK):
-                nc.tensor.matmul(
-                    bank[:, r, :], neg[:, r * P : (r + 1) * P], ident[:], start=(r == 0), stop=False, is_transpose=True
-                )
-
-        def gather_vals(c):
-            picked_vals = held(f"picked_vals{c}", [P, I], F32)
-            gather(picked_vals[:], val_pool[c])
-            open_err(c)
-            for r in range(PACK):
-                nc.tensor.matmul(
-                    err_banks[c][0][:, r, :],
-                    picked_vals[:, r * P : (r + 1) * P],
-                    ident[:],
-                    start=False,
-                    stop=(r == PACK - 1),
-                    is_transpose=True,
-                )
+            terms = (minus_b[c], picked_vals[c])
+            for n, term in enumerate(terms):
+                for r in range(PACK):
+                    nc.tensor.matmul(
+                        bank[:, r, :],
+                        term[:, r * P : (r + 1) * P],
+                        ident[:],
+                        start=(n == 0 and r == 0),
+                        stop=(n == 1 and r == PACK - 1),
+                        is_transpose=True,
+                    )
+            err_banks.append(bank)
 
         out_rows = out.rearrange("(p t) e -> p t e", t=PACK)
         predict(0)
         predict(1)
-        gather_vals(0)
-        interleave(nc.scalar.copy, state_grouped[1][:], state_raw[1][:])
-        ks_q.append(scale_and_quantize(f"ks{PACK - 1}", key_banks[PACK - 1], step_wide))
-        state_q.append(quantize("state1", state_grouped[1], HALF))
+        turn_err(0)
+        state_q.append(quantize("state1", state_grouped[1], HALF, VAL_AT[0] + POOL_BYTES // 2))
+        ks.append(scale("ks3", key_banks[3], step_wide, VAL_AT[0]))
         predict(2)
         predict(3)
-        for c in range(blocks):
+
+        def update(c, es_q):
             if c + 1 < blocks:
-                gather_vals(c + 1)
-            es_q = scale_and_quantize(f"es{c}", err_banks[c][0], vsc_wide)
-            acc = psum.tile([P, PACK, P], F32, name=f"update{c}", tag="update", bufs=2)
-            for t in range(PACK):
-                product(acc[:, t, :], ks_q[t], slice(0, P), es_q)
-            result = held(f"result{c}", [P, PACK, P], F32)
-            nc.scalar.copy(out=result[:], in_=acc[:])
-            nc.sync.dma_start(out=out_rows[:, :, c * P : (c + 1) * P], in_=result[:])
+                parts = [(range(PACK), "update", nc.scalar.copy, nc.sync)]
+            else:
+                parts = [(range(2), "update", nc.vector.tensor_copy, nc.sync), (range(2, PACK), "b", nc.scalar.copy, nc.scalar)]
+            for planes, tag, copy, queue in parts:
+                first = planes[0]
+                acc = psum.tile([P, len(planes), P], F32, name=f"update{c}_{first}", tag=tag, bufs=2)
+                for t in planes:
+                    product(acc[:, t - first, :], ks_q[t], slice(0, P), es_q)
+                result = held(f"result{c}_{first}", [P, len(planes), P], F32)
+                copy(out=result[:], in_=acc[:])
+                queue.dma_start(out=out_rows[:, first : first + len(planes), c * P : (c + 1) * P], in_=result[:])
+
+        es = []
+        for c in range(blocks - 1):
+            gather_vals(c + 1)
+            turn_err(c + 1)
+            if c == 0:
+                ks_q.append(quantize("ks3", ks[3], P, VAL_AT[1] + POOL_BYTES // 2))
+            else:
+                update(c - 1, quantize(f"es{c - 1}", es[c - 1], P, VAL_AT[c + 1] + POOL_BYTES // 2))
+            es.append(scale(f"es{c}", err_banks[c], vsc_wide, VAL_AT[c + 1]))
+        update(blocks - 2, quantize(f"es{blocks - 2}", es[blocks - 2], P))
+        update(blocks - 1, quantize(f"es{blocks - 1}", scale(f"es{blocks - 1}", err_banks[blocks - 1], vsc_wide), P))

@@ -98,17 +98,14 @@ def tile_attend_deltastep_kernel(tc, state, keys, vals, step, vsc, dsc, offs, ou
         step_wide = slot_cols[:, 0:PACK].unsqueeze(1).to_broadcast([P, P, PACK])
         vsc_wide = slot_cols[:, PACK : 2 * PACK].unsqueeze(1).to_broadcast([P, P, PACK])
 
-        picked = held("picked", [P, PACK, I], F32)
+        picked = [held(f"picked{h}", [P, 2, I], F32) for h in range(2)]
         key_banks, ks_q = [], []
 
         def turn_keys(t):
             scaled = held(f"scaled{t}", [P, I], F32)
-            if t < PACK - 1:
-                nc.scalar.activation(out=scaled[:], in_=picked[:, t, :], func=COPY, scale=dsc_cols[:, t : t + 1])
-            else:
-                nc.vector.tensor_scalar(
-                    out=scaled[:], in0=picked[:, t, :], scalar1=dsc_cols[:, t : t + 1], scalar2=None, op0=MULT
-                )
+            nc.scalar.activation(
+                out=scaled[:], in_=picked[t // 2][:, t % 2, :], func=COPY, scale=dsc_cols[:, t : t + 1]
+            )
             bank = psum.tile([P, PACK, P], F32, name=f"key_turn{t}", tag="turn", bufs=4)
             for r in range(PACK):
                 nc.tensor.transpose(bank[:, r, :], scaled[:, r * P : (r + 1) * P], ident[:])
@@ -119,39 +116,43 @@ def tile_attend_deltastep_kernel(tc, state, keys, vals, step, vsc, dsc, offs, ou
             nc.vector.tensor_tensor(out=grouped[:], in0=bank[:].rearrange("s r x -> s x r"), in1=wide, op=MULT)
             return grouped
 
-        ks = []
-        for t in range(PACK):
-            gather(picked[:, t, :], key_pool[t])
-            if t > 1:
-                ks_q.append(quantize(f"ks{t - 2}", ks[t - 2], P, KEY_AT[t] + POOL_BYTES // 2))
-            turn_keys(t)
-            if t > 0:
-                ks.append(scale(f"ks{t - 1}", key_banks[t - 1], step_wide, KEY_AT[t]))
-
         def interleave(copy, dst, src):
             copy(out=dst.rearrange("p (c i) t -> p c t i", i=4), in_=src.rearrange("p t (c i) -> p c t i", i=4))
 
         keys_grouped = held("keys_grouped", [P, I, PACK], BF16, KEYS_GROUPED_AT)
+        ks = []
+        for t in range(PACK):
+            gather(picked[t // 2][:, t % 2, :], key_pool[t])
+            if t > 1:
+                ks_q.append(quantize(f"ks{t - 2}", ks[t - 2], P, KEY_AT[t] + POOL_BYTES // 2))
+            turn_keys(t)
+            if t % 2 == 1:
+                interleave(nc.scalar.copy, keys_grouped[:, :, t - 1 : t + 1], picked[t // 2][:])
+            if t > 0:
+                ks.append(scale(f"ks{t - 1}", key_banks[t - 1], step_wide, KEY_AT[t]))
+
         state_grouped = [held(f"state_grouped{h}", [P, HALF, PACK], BF16, KEY_AT[2] if h == 0 else None) for h in range(2)]
-        interleave(nc.scalar.copy, keys_grouped[:], picked[:])
         interleave(nc.vector.tensor_copy, state_grouped[0][:], state_raw[0][:])
+        interleave(nc.scalar.copy, state_grouped[1][:], state_raw[1][:])
         ks_q.append(quantize("ks2", ks[2], P, STATE_AT[0]))
         state_q = [quantize("state0", state_grouped[0], HALF)]
+        keys_q = quantize("keys", keys_grouped, I)
+        ks.append(scale("ks3", key_banks[3], step_wide))
+        state_q.append(quantize("state1", state_grouped[1], HALF))
         picked_vals = []
 
         def gather_vals(c, at=None):
             picked_vals.append(held(f"picked_vals{c}", [P, I], F32, at))
             gather(picked_vals[c][:], val_pool[c])
 
-        keys_q = quantize("keys", keys_grouped, I)
         gather_vals(0, KEYS_GROUPED_AT)
-        interleave(nc.scalar.copy, state_grouped[1][:], state_raw[1][:])
+        ks_q.append(quantize("ks3", ks[3], P, VAL_AT[0]))
 
         blocks = E // P
         minus_b, err_banks = [], []
 
         def predict(c):
-            acc = psum.tile([P, I], F32, name=f"b{c}", tag="b", bufs=2)
+            acc = psum.tile([P, I], F32, name=f"b{c}", tag="b" if c < 2 else "update", bufs=2)
             product(acc[:], state_q[c // 2], slice(c % 2 * P, (c % 2 + 1) * P), keys_q)
             neg = held(f"minus_b{c}", [P, I], F32, STATE_AT[1] if c == 0 else None)
             nc.scalar.activation(out=neg[:], in_=acc[:], func=COPY, scale=-1.0)
@@ -173,13 +174,9 @@ def tile_attend_deltastep_kernel(tc, state, keys, vals, step, vsc, dsc, offs, ou
             err_banks.append(bank)
 
         out_rows = out.rearrange("(p t) e -> p t e", t=PACK)
-        predict(0)
-        predict(1)
+        for c in range(blocks):
+            predict(c)
         turn_err(0)
-        state_q.append(quantize("state1", state_grouped[1], HALF, VAL_AT[0] + POOL_BYTES // 2))
-        ks.append(scale("ks3", key_banks[3], step_wide, VAL_AT[0]))
-        predict(2)
-        predict(3)
 
         def update(c, es_q):
             if c + 1 < blocks:
@@ -195,14 +192,25 @@ def tile_attend_deltastep_kernel(tc, state, keys, vals, step, vsc, dsc, offs, ou
                 copy(out=result[:], in_=acc[:])
                 queue.dma_start(out=out_rows[:, first : first + len(planes), c * P : (c + 1) * P], in_=result[:])
 
-        es = []
-        for c in range(blocks - 1):
-            gather_vals(c + 1)
-            turn_err(c + 1)
-            if c == 0:
-                ks_q.append(quantize("ks3", ks[3], P, VAL_AT[1] + POOL_BYTES // 2))
-            else:
-                update(c - 1, quantize(f"es{c - 1}", es[c - 1], P, VAL_AT[c + 1] + POOL_BYTES // 2))
-            es.append(scale(f"es{c}", err_banks[c], vsc_wide, VAL_AT[c + 1]))
-        update(blocks - 2, quantize(f"es{blocks - 2}", es[blocks - 2], P))
-        update(blocks - 1, quantize(f"es{blocks - 1}", scale(f"es{blocks - 1}", err_banks[blocks - 1], vsc_wide), P))
+        def scale_on_scalar(c):
+            flat = held(f"es_flat{c}", [P, PACK, P], F32)
+            for r in range(PACK):
+                nc.scalar.activation(
+                    out=flat[:, r, :], in_=err_banks[c][:, r, :], func=COPY, scale=slot_cols[:, PACK + r : PACK + r + 1]
+                )
+            grouped = held(f"es{c}", [P, P, PACK], BF16)
+            interleave(nc.scalar.copy, grouped[:], flat[:])
+            return grouped
+
+        es0 = scale_on_scalar(0)
+        gather_vals(1)
+        turn_err(1)
+        gather_vals(2)
+        turn_err(2)
+        es1 = scale("es1", err_banks[1], vsc_wide, VAL_AT[2])
+        update(0, quantize("es0", es0, P, VAL_AT[2] + POOL_BYTES // 2))
+        gather_vals(3)
+        turn_err(3)
+        update(1, quantize("es1", es1, P, VAL_AT[3] + POOL_BYTES // 2))
+        update(2, quantize("es2", scale("es2", err_banks[2], vsc_wide, VAL_AT[3]), P))
+        update(3, quantize("es3", scale("es3", err_banks[3], vsc_wide), P))

@@ -182,10 +182,15 @@ def tile_attend_deltastep_kernel(tc, state, keys, vals, step, vsc, dsc, offs, ou
             if c + 1 < blocks:
                 parts = [(range(PACK), "update", nc.scalar.copy, nc.sync)]
             else:
-                parts = [(range(2), "update", nc.vector.tensor_copy, nc.sync), (range(2, PACK), "b", nc.scalar.copy, nc.scalar)]
+                parts = [
+                    (range(0, 1), "b", nc.vector.tensor_copy, nc.sync),
+                    (range(1, 2), "b", nc.scalar.copy, nc.scalar),
+                    (range(2, 3), "turn", nc.vector.tensor_copy, nc.sync),
+                    (range(3, 4), "turn", nc.scalar.copy, nc.scalar),
+                ]
             for planes, tag, copy, queue in parts:
                 first = planes[0]
-                acc = psum.tile([P, len(planes), P], F32, name=f"update{c}_{first}", tag=tag, bufs=2)
+                acc = psum.tile([P, len(planes), P], F32, name=f"update{c}_{first}", tag=tag, bufs=4 if tag == "turn" else 2)
                 for t in planes:
                     product(acc[:, t - first, :], ks_q[t], slice(0, P), es_q)
                 result = held(f"result{c}_{first}", [P, len(planes), P], F32)
@@ -209,8 +214,8 @@ def tile_attend_deltastep_kernel(tc, state, keys, vals, step, vsc, dsc, offs, ou
         turn_err(2)
         es1 = scale("es1", err_banks[1], vsc_wide, VAL_AT[2])
         update(0, quantize("es0", es0, P, VAL_AT[2] + POOL_BYTES // 2))
+        update(1, quantize("es1", es1, P))
         gather_vals(3)
         turn_err(3)
-        update(1, quantize("es1", es1, P, VAL_AT[3] + POOL_BYTES // 2))
         update(2, quantize("es2", scale("es2", err_banks[2], vsc_wide, VAL_AT[3]), P))
         update(3, quantize("es3", scale("es3", err_banks[3], vsc_wide), P))

from contextlib import ExitStack

import concourse.mybir as mybir
from concourse.masks import make_identity

D, T, I, E = 512, 2048, 512, 512
FLOPS = 2 * D * I * E + 2 * I * D * E

F32 = mybir.dt.float32
BF16 = mybir.dt.bfloat16
U32 = mybir.dt.uint32
U16 = mybir.dt.uint16
U8 = mybir.dt.uint8
FP8X4 = mybir.dt.float8_e4m3fn_x4
COPY = mybir.ActivationFunctionType.Copy
MULT = mybir.AluOpType.mult

P = 128
PACK = 4
RUN = 8
HALF = 256
POOL_BYTES = 4 * T
GROUPED_BYTES = 2 * PACK * P
STATE_BYTES = 4 * PACK * HALF
KEY_AT = [0, POOL_BYTES, 2 * POOL_BYTES + STATE_BYTES, 3 * POOL_BYTES + STATE_BYTES]
VAL_AT = [KEY_AT[3] + (1 + c) * POOL_BYTES for c in range(E // P)]
STATE_AT = [2 * POOL_BYTES, VAL_AT[3] + POOL_BYTES]
KEYS_GROUPED_AT = STATE_AT[1] + STATE_BYTES


def tile_attend_deltastep_kernel(tc, state, keys, vals, step, vsc, dsc, offs, out):
    nc = tc.nc
    with ExitStack() as ctx:
        keep = ctx.enter_context(tc.tile_pool(name="keep", bufs=1))
        placed = ctx.enter_context(tc.tile_pool(name="placed", bufs=1))
        psum = ctx.enter_context(tc.psum_pool(name="psum", bufs=1))

        def held(name, shape, dtype, at=None):
            if at is None:
                return keep.tile(shape, dtype, name=name, align_bytes=64)
            return placed.tile(shape, dtype, name=name, align_bytes=64, offset=at)

        def gather(dst, window):
            nc.vector.tensor_copy(
                out=dst.bitcast(U32).rearrange("p (r g j) -> p g r j", r=PACK, j=RUN),
                in_=window[:].bitcast(U32).indirect(offsets[:]),
            )

        def quantize(name, grouped, width, after=None):
            codes = held(name + "_codes", [P, width], U32)
            scales = held(name + "_scales", [P, width], U8, after)
            nc.vector.quantize_mx(
                out=codes[:].bitcast(FP8X4), scales=scales[:], in_=grouped[:].rearrange("p w j -> p (w j)")
            )
            return codes, scales

        def product(acc, lhs, lhs_cols, rhs):
            nc.tensor.matmul_mx(
                out=acc,
                lhsT=lhs[0][:, lhs_cols].bitcast(FP8X4),
                lhsT_scale=lhs[1][:, lhs_cols],
                rhs=rhs[0][:].bitcast(FP8X4),
                rhs_scale=rhs[1][:],
                start=True,
                stop=True,
            )

        slot_rows = held("slot_rows", [P, P], F32)
        nc.gpsimd.memset(slot_rows[:], 0.0)
        ident = held("ident", [P, P], F32)
        make_identity(nc, ident[:])
        offsets = keep.tile([P, I // 16], U16, name="offsets")
        keys_planes = keys.rearrange("(p t) c -> t p c", t=PACK)
        key_pool = [held(f"key_pool{t}", [P, T], F32, KEY_AT[t]) for t in range(PACK)]
        val_pool = [held(f"val_pool{c}", [P, T], F32, VAL_AT[c]) for c in range(E // P)]
        state_raw = [held(f"state_raw{h}", [P, PACK, HALF], F32, STATE_AT[h]) for h in range(2)]
        state_rows = state.rearrange("(p t) e -> p t e", t=PACK)
        nc.sync.dma_start(out=key_pool[0][:], in_=keys_planes[0])
        nc.sync.dma_start(offsets[:], offs)
        dsc_cols = held("dsc_cols", [P, PACK], F32)
        nc.sync.dma_start(out=dsc_cols[:], in_=dsc.rearrange("o (p t) -> p (o t)", t=PACK))
        for n, vec in enumerate((step, vsc)):
            nc.sync.dma_start(
                out=slot_rows[n * PACK : (n + 1) * PACK, :].rearrange("r (g j) -> r g j", j=RUN),
                in_=vec.rearrange("(g r j) o -> r g (j o)", r=PACK, j=RUN),
            )
        for t in range(1, PACK):
            nc.sync.dma_start(out=key_pool[t][:], in_=keys_planes[t])
        for h in range(2):
            nc.sync.dma_start(out=state_raw[h][:], in_=state_rows[:, :, h * HALF : (h + 1) * HALF])
        for c in range(E // P):
            nc.sync.dma_start(out=val_pool[c][:], in_=vals[c * P : (c + 1) * P, :])

        turned = psum.tile([P, PACK, P], F32, name="slot_turn", tag="turn", bufs=4)
        nc.tensor.transpose(turned[:, 0, :], slot_rows[:], ident[:])
        slot_cols = held("slot_cols", [P, 2 * PACK], F32)
        nc.scalar.copy(out=slot_cols[:], in_=turned[:, 0, 0 : 2 * PACK])
        step_wide = slot_cols[:, 0:PACK].unsqueeze(1).to_broadcast([P, P, PACK])
        vsc_wide = slot_cols[:, PACK : 2 * PACK].unsqueeze(1).to_broadcast([P, P, PACK])

        picked = [held(f"picked{h}", [P, 2, I], F32) for h in range(2)]
        key_banks, ks_q = [], []

        def turn_keys(t):
            scaled = held(f"scaled{t}", [P, I], F32)
            nc.scalar.activation(
                out=scaled[:], in_=picked[t // 2][:, t % 2, :], func=COPY, scale=dsc_cols[:, t : t + 1]
            )
            bank = psum.tile([P, PACK, P], F32, name=f"key_turn{t}", tag="turn", bufs=4)
            for r in range(PACK):
                nc.tensor.transpose(bank[:, r, :], scaled[:, r * P : (r + 1) * P], ident[:])
            key_banks.append(bank)

        def scale(name, bank, wide, at=None):
            grouped = held(name, [P, P, PACK], BF16, at)
            nc.vector.tensor_tensor(out=grouped[:], in0=bank[:].rearrange("s r x -> s x r"), in1=wide, op=MULT)
            return grouped

        def interleave(copy, dst, src):
            copy(out=dst.rearrange("p (c i) t -> p c t i", i=4), in_=src.rearrange("p t (c i) -> p c t i", i=4))

        keys_grouped = held("keys_grouped", [P, I, PACK], BF16, KEYS_GROUPED_AT)
        ks = []
        for t in range(PACK):
            gather(picked[t // 2][:, t % 2, :], key_pool[t])
            if t > 1:
                ks_q.append(quantize(f"ks{t - 2}", ks[t - 2], P, KEY_AT[t] + POOL_BYTES // 2))
            turn_keys(t)
            if t % 2 == 1:
                interleave(nc.scalar.copy, keys_grouped[:, :, t - 1 : t + 1], picked[t // 2][:])
            if t > 0:
                ks.append(scale(f"ks{t - 1}", key_banks[t - 1], step_wide, KEY_AT[t]))

        state_grouped = [held(f"state_grouped{h}", [P, HALF, PACK], BF16, KEY_AT[2] if h == 0 else None) for h in range(2)]
        interleave(nc.vector.tensor_copy, state_grouped[0][:], state_raw[0][:])
        interleave(nc.scalar.copy, state_grouped[1][:], state_raw[1][:])
        ks_q.append(quantize("ks2", ks[2], P, STATE_AT[0]))
        state_q = [quantize("state0", state_grouped[0], HALF)]
        keys_q = quantize("keys", keys_grouped, I)
        ks.append(scale("ks3", key_banks[3], step_wide))
        state_q.append(quantize("state1", state_grouped[1], HALF))
        picked_vals = []

        def gather_vals(c, at=None):
            picked_vals.append(held(f"picked_vals{c}", [P, I], F32, at))
            gather(picked_vals[c][:], val_pool[c])

        gather_vals(0, KEYS_GROUPED_AT)
        ks_q.append(quantize("ks3", ks[3], P, VAL_AT[0]))

        blocks = E // P
        minus_b, err_banks = [], []

        def predict(c):
            acc = psum.tile([P, I], F32, name=f"b{c}", tag="b" if c < 2 else "update", bufs=2)
            product(acc[:], state_q[c // 2], slice(c % 2 * P, (c % 2 + 1) * P), keys_q)
            neg = held(f"minus_b{c}", [P, I], F32, STATE_AT[1] if c == 0 else None)
            nc.scalar.activation(out=neg[:], in_=acc[:], func=COPY, scale=-1.0)
            minus_b.append(neg)

        def turn_err(c):
            bank = psum.tile([P, PACK, P], F32, name=f"err{c}", tag="turn", bufs=4)
            terms = (minus_b[c], picked_vals[c])
            for n, term in enumerate(terms):
                for r in range(PACK):
                    nc.tensor.matmul(
                        bank[:, r, :],
                        term[:, r * P : (r + 1) * P],
                        ident[:],
                        start=(n == 0 and r == 0),
                        stop=(n == 1 and r == PACK - 1),
                        is_transpose=True,
                    )
            err_banks.append(bank)

        out_rows = out.rearrange("(p t) e -> p t e", t=PACK)
        for c in range(blocks):
            predict(c)
        turn_err(0)

        def update(c, es_q):
            if c + 1 < blocks:
                parts = [(range(PACK), "update", nc.scalar.copy, nc.sync)]
            else:
                parts = [
                    (range(0, 1), "b", nc.vector.tensor_copy, nc.sync),
                    (range(1, 2), "b", nc.scalar.copy, nc.scalar),
                    (range(2, 3), "turn", nc.vector.tensor_copy, nc.sync),
                    (range(3, 4), "turn", nc.scalar.copy, nc.scalar),
                ]
            for planes, tag, copy, queue in parts:
                first = planes[0]
                acc = psum.tile([P, len(planes), P], F32, name=f"update{c}_{first}", tag=tag, bufs=4 if tag == "turn" else 2)
                for t in planes:
                    product(acc[:, t - first, :], ks_q[t], slice(0, P), es_q)
                result = held(f"result{c}_{first}", [P, len(planes), P], F32)
                copy(out=result[:], in_=acc[:])
                queue.dma_start(out=out_rows[:, first : first + len(planes), c * P : (c + 1) * P], in_=result[:])

        def scale_on_scalar(c):
            flat = held(f"es_flat{c}", [P, PACK, P], F32)
            for r in range(PACK):
                nc.scalar.activation(
                    out=flat[:, r, :], in_=err_banks[c][:, r, :], func=COPY, scale=slot_cols[:, PACK + r : PACK + r + 1]
                )
            grouped = held(f"es{c}", [P, P, PACK], BF16)
            interleave(nc.scalar.copy, grouped[:], flat[:])
            return grouped

        es0 = scale_on_scalar(0)
        gather_vals(1)
        turn_err(1)
        gather_vals(2)
        turn_err(2)
        es1 = scale("es1", err_banks[1], vsc_wide, VAL_AT[2])
        update(0, quantize("es0", es0, P, VAL_AT[2] + POOL_BYTES // 2))
        update(1, quantize("es1", es1, P))
        gather_vals(3)
        turn_err(3)
        update(2, quantize("es2", scale("es2", err_banks[2], vsc_wide, VAL_AT[3]), P))
        update(3, quantize("es3", scale("es3", err_banks[3], vsc_wide), P))
